import numpy as np, ml_dtypes
CORES = [102,230,358,486]
N = 4
ROOT = 0
def setup_inputs(rng):
    return {"x": rng.standard_normal((N, 128, N * 512), dtype=np.float32).astype(ml_dtypes.bfloat16)}
def reference(x):
    return {"y": np.stack([x[ROOT][:, r * 512:(r + 1) * 512] for r in range(N)])}

@@ -1,0 +1,44 @@
+import concourse.bass as bass
+SCRATCH = {'a': ('dram', [128, 512], 'bfloat16'), 'b': ('dram', [4, 128, 128], 'bfloat16'), 'c': ('dram', [4, 128, 128], 'bfloat16')}
+SEMAPHORES = ['ld_a', 'ld_b', 'ld_c', 'st', 'sent', 'got']
+ALL8 = 255
+
+def rank_program(g, core, T, topo):
+    root, r1, r2, r3 = T.cores
+    chip_h1 = r1 - r1 % 8
+    chip_h0 = root - root % 8
+    relays = [chip_h1 + 0, chip_h1 + 4, chip_h1 + 2, chip_h1 + 7]
+    helpers = [None, chip_h0 + 0, chip_h0 + 2, chip_h0 + 4]
+    S = T.sem
+
+    def to(d):
+        rid, pid = topo.addr(d, core)
+        return bass.DstId(rid=rid, pnc=pid)
+    if core == root:
+        g.dma_start(T.c[:], T.x[:, 1024:1536]).then_inc(S.ld_c, 16)
+        g.dma_start(T.b[:], T.x[:, 1536:2048]).then_inc(S.ld_b, 16)
+        g.dma_start(T.a[:], T.x[:, 512:1024]).then_inc(S.ld_a, 16)
+        g.wait_ge(S.ld_c, 16)
+        g.remote_dma_fused([bass.RemoteDMATransfer(dst_ids=[to(rl)], dma_engine_mask=3 << 2 * q, remote_sem=S.got, src=T.c[q], dst=T.c[q]) for q, rl in enumerate(relays)], local_sem=S.sent)
+        g.wait_ge(S.ld_b, 16)
+        g.remote_dma_fused([bass.RemoteDMATransfer(dst_ids=[to(r3)], dma_engine_mask=240, remote_sem=S.got, src=T.b[0], dst=T.b[0])] + [bass.RemoteDMATransfer(dst_ids=[to(helpers[q])], dma_engine_mask=3 << 6 + 2 * q, remote_sem=S.got, src=T.b[q], dst=T.b[q]) for q in (1, 2, 3)], local_sem=S.sent)
+        g.wait_ge(S.ld_a, 16)
+        rid, pid = topo.addr(r1, core)
+        g.remote_dma(T.a[:], T.a[:], S.got, S.sent, pid, rid, ALL8)
+        g.dma_start(T.y[:], T.x[:, 0:512]).then_inc(S.st, 16)
+        g.wait_ge(S.sent, 26)
+        g.wait_ge(S.st, 16)
+    elif core in relays or core in helpers:
+        if core in relays:
+            buf, q, d = (T.c, relays.index(core), r2)
+        else:
+            buf, q, d = (T.b, helpers.index(core), r3)
+        rid, pid = topo.addr(d, core)
+        g.wait_ge(S.got, 2)
+        g.remote_dma(buf[q], buf[q], S.got, S.sent, pid, rid, ALL8)
+        g.wait_ge(S.sent, 8)
+    elif core in (r1, r2, r3):
+        buf, n = {r1: (T.a, 8), r2: (T.c, 32), r3: (T.b, 28)}[core]
+        g.wait_ge(S.got, n)
+        g.dma_start(T.y[:], buf[:]).then_inc(S.st, 16)
+        g.wait_ge(S.st, 16)

@@ -3,6 +3,7 @@ SCRATCH = {'a': ('dram', [128, 512], 'bfloat16'), 'b': ('dram', [4, 128, 128], '
 SEMAPHORES = ['ld_a', 'ld_b', 'ld_c', 'st', 'sent', 'got']
 ALL8 = 255
 
+
 def rank_program(g, core, T, topo):
     root, r1, r2, r3 = T.cores
     chip_h1 = r1 - r1 % 8
@@ -15,9 +16,10 @@ def rank_program(g, core, T, topo):
         rid, pid = topo.addr(d, core)
         return bass.DstId(rid=rid, pnc=pid)
     if core == root:
-        g.dma_start(T.c[:], T.x[:, 1024:1536]).then_inc(S.ld_c, 16)
-        g.dma_start(T.b[:], T.x[:, 1536:2048]).then_inc(S.ld_b, 16)
-        g.dma_start(T.a[:], T.x[:, 512:1024]).then_inc(S.ld_a, 16)
+        g.sync.dma_start(T.c[:], T.x[:, 1024:1536]).then_inc(S.ld_c, 16)
+        g.scalar.dma_start(T.b[:], T.x[:, 1536:2048]).then_inc(S.ld_b, 16)
+        g.sync.dma_start(T.a[:], T.x[:, 512:1024]).then_inc(S.ld_a, 16)
+        g.scalar.dma_start(T.y[:], T.x[:, 0:512]).then_inc(S.st, 16)
         g.wait_ge(S.ld_c, 16)
         g.remote_dma_fused([bass.RemoteDMATransfer(dst_ids=[to(rl)], dma_engine_mask=3 << 2 * q, remote_sem=S.got, src=T.c[q], dst=T.c[q]) for q, rl in enumerate(relays)], local_sem=S.sent)
         g.wait_ge(S.ld_b, 16)
@@ -25,7 +27,6 @@ def rank_program(g, core, T, topo):
         g.wait_ge(S.ld_a, 16)
         rid, pid = topo.addr(r1, core)
         g.remote_dma(T.a[:], T.a[:], S.got, S.sent, pid, rid, ALL8)
-        g.dma_start(T.y[:], T.x[:, 0:512]).then_inc(S.st, 16)
         g.wait_ge(S.sent, 26)
         g.wait_ge(S.st, 16)
     elif core in relays or core in helpers:
@@ -39,6 +40,6 @@ def rank_program(g, core, T, topo):
         g.wait_ge(S.sent, 8)
     elif core in (r1, r2, r3):
         buf, n = {r1: (T.a, 8), r2: (T.c, 32), r3: (T.b, 28)}[core]
-        g.wait_ge(S.got, n)
-        g.dma_start(T.y[:], buf[:]).then_inc(S.st, 16)
+        g.sync.wait_ge(S.got, n)
+        g.sync.dma_start(T.y[:], buf[:]).then_inc(S.st, 16)
         g.wait_ge(S.st, 16)

@@ -1,6 +1,6 @@
 import concourse.bass as bass
-SCRATCH = {'a': ('dram', [128, 512], 'bfloat16'), 'b': ('dram', [4, 128, 128], 'bfloat16'), 'c': ('dram', [4, 128, 128], 'bfloat16')}
-SEMAPHORES = ['ld_a', 'ld_b', 'ld_c', 'st', 'sent', 'got']
+SCRATCH = {'a': ('dram', [128, 512], 'bfloat16'), 'b': ('dram', [8, 128, 64], 'bfloat16'), 'c': ('dram', [8, 128, 64], 'bfloat16')}
+SEMAPHORES = ['ld0', 'ld1', 'ld_a', 'st', 'sent', 'got0', 'got1']
 ALL8 = 255
 
 
@@ -9,25 +9,31 @@ def rank_program(g, core, T, topo):
     chip_h1 = r1 - r1 % 8
     chip_h0 = root - root % 8
     relays = [chip_h1 + 0, chip_h1 + 4, chip_h1 + 2, chip_h1 + 7]
-    helpers = [None, chip_h0 + 0, chip_h0 + 2, chip_h0 + 4]
+    helpers = [chip_h0 + 0, chip_h0 + 2, chip_h0 + 4, chip_h0 + 7]
     S = T.sem
+    got = [S.got0, S.got1]
 
     def to(d):
         rid, pid = topo.addr(d, core)
         return bass.DstId(rid=rid, pnc=pid)
     if core == root:
-        g.sync.dma_start(T.c[:], T.x[:, 1024:1536]).then_inc(S.ld_c, 16)
-        g.scalar.dma_start(T.b[:], T.x[:, 1536:2048]).then_inc(S.ld_b, 16)
+        g.sync.dma_start(T.c[0:4], T.x[0:64, 1024:1536]).then_inc(S.ld0, 16)
+        g.scalar.dma_start(T.b[0:4], T.x[0:64, 1536:2048]).then_inc(S.ld0, 16)
+        g.sync.dma_start(T.c[4:8], T.x[64:128, 1024:1536]).then_inc(S.ld1, 16)
+        g.scalar.dma_start(T.b[4:8], T.x[64:128, 1536:2048]).then_inc(S.ld1, 16)
         g.sync.dma_start(T.a[:], T.x[:, 512:1024]).then_inc(S.ld_a, 16)
-        g.scalar.dma_start(T.y[:], T.x[:, 0:512]).then_inc(S.st, 16)
-        g.wait_ge(S.ld_c, 16)
-        g.remote_dma_fused([bass.RemoteDMATransfer(dst_ids=[to(rl)], dma_engine_mask=3 << 2 * q, remote_sem=S.got, src=T.c[q], dst=T.c[q]) for q, rl in enumerate(relays)], local_sem=S.sent)
-        g.wait_ge(S.ld_b, 16)
-        g.remote_dma_fused([bass.RemoteDMATransfer(dst_ids=[to(r3)], dma_engine_mask=240, remote_sem=S.got, src=T.b[0], dst=T.b[0])] + [bass.RemoteDMATransfer(dst_ids=[to(helpers[q])], dma_engine_mask=3 << 6 + 2 * q, remote_sem=S.got, src=T.b[q], dst=T.b[q]) for q in (1, 2, 3)], local_sem=S.sent)
+        for h, ld in enumerate((S.ld0, S.ld1)):
+            g.wait_ge(ld, 32)
+            g.remote_dma_fused(
+                [bass.RemoteDMATransfer(dst_ids=[to(rl)], dma_engine_mask=3 << 2 * q, remote_sem=got[h], src=T.c[4 * h + q], dst=T.c[4 * h + q]) for q, rl in enumerate(relays)]
+                + [bass.RemoteDMATransfer(dst_ids=[to(hp)], dma_engine_mask=3 << 8 + 2 * q, remote_sem=got[h], src=T.b[4 * h + q], dst=T.b[4 * h + q]) for q, hp in enumerate(helpers)],
+                local_sem=S.sent)
         g.wait_ge(S.ld_a, 16)
         rid, pid = topo.addr(r1, core)
-        g.remote_dma(T.a[:], T.a[:], S.got, S.sent, pid, rid, ALL8)
-        g.wait_ge(S.sent, 26)
+        g.remote_dma(T.a[:], T.a[:], S.got0, S.sent, pid, rid, ALL8)
+        g.scalar.wait_ge(S.sent, 40)
+        g.scalar.dma_start(T.y[:], T.x[:, 0:512]).then_inc(S.st, 16)
+        g.wait_ge(S.sent, 40)
         g.wait_ge(S.st, 16)
     elif core in relays or core in helpers:
         if core in relays:
@@ -35,11 +41,18 @@ def rank_program(g, core, T, topo):
         else:
             buf, q, d = (T.b, helpers.index(core), r3)
         rid, pid = topo.addr(d, core)
-        g.wait_ge(S.got, 2)
-        g.remote_dma(buf[q], buf[q], S.got, S.sent, pid, rid, ALL8)
-        g.wait_ge(S.sent, 8)
-    elif core in (r1, r2, r3):
-        buf, n = {r1: (T.a, 8), r2: (T.c, 32), r3: (T.b, 28)}[core]
-        g.sync.wait_ge(S.got, n)
-        g.sync.dma_start(T.y[:], buf[:]).then_inc(S.st, 16)
+        for h in (0, 1):
+            g.wait_ge(got[h], 2)
+            g.remote_dma(buf[4 * h + q], buf[4 * h + q], got[h], S.sent, pid, rid, ALL8)
+        g.wait_ge(S.sent, 16)
+    elif core == r1:
+        g.sync.wait_ge(S.got0, 8)
+        g.sync.dma_start(T.y[:], T.a[:]).then_inc(S.st, 16)
         g.wait_ge(S.st, 16)
+    elif core in (r2, r3):
+        buf = T.c if core == r2 else T.b
+        g.sync.wait_ge(S.got0, 32)
+        g.sync.dma_start(T.y[0:64, :], buf[0:4]).then_inc(S.st, 16)
+        g.scalar.wait_ge(S.got1, 32)
+        g.scalar.dma_start(T.y[64:128, :], buf[4:8]).then_inc(S.st, 16)
+        g.wait_ge(S.st, 32)

import concourse.bass as bass
SCRATCH = {'a': ('dram', [128, 512], 'bfloat16'), 'b': ('dram', [8, 128, 64], 'bfloat16'), 'c': ('dram', [8, 128, 64], 'bfloat16')}
SEMAPHORES = ['ld0', 'ld1', 'ld_a', 'st', 'sent', 'got0', 'got1']
ALL8 = 255


def rank_program(g, core, T, topo):
    root, r1, r2, r3 = T.cores
    chip_h1 = r1 - r1 % 8
    chip_h0 = root - root % 8
    relays = [chip_h1 + 0, chip_h1 + 4, chip_h1 + 2, chip_h1 + 7]
    helpers = [chip_h0 + 0, chip_h0 + 2, chip_h0 + 4, chip_h0 + 7]
    S = T.sem
    got = [S.got0, S.got1]

    def to(d):
        rid, pid = topo.addr(d, core)
        return bass.DstId(rid=rid, pnc=pid)
    if core == root:
        g.sync.dma_start(T.c[0:4], T.x[0:64, 1024:1536]).then_inc(S.ld0, 16)
        g.scalar.dma_start(T.b[0:4], T.x[0:64, 1536:2048]).then_inc(S.ld0, 16)
        g.sync.dma_start(T.c[4:8], T.x[64:128, 1024:1536]).then_inc(S.ld1, 16)
        g.scalar.dma_start(T.b[4:8], T.x[64:128, 1536:2048]).then_inc(S.ld1, 16)
        g.sync.dma_start(T.a[:], T.x[:, 512:1024]).then_inc(S.ld_a, 16)
        for h, ld in enumerate((S.ld0, S.ld1)):
            g.wait_ge(ld, 32)
            g.remote_dma_fused(
                [bass.RemoteDMATransfer(dst_ids=[to(rl)], dma_engine_mask=3 << 2 * q, remote_sem=got[h], src=T.c[4 * h + q], dst=T.c[4 * h + q]) for q, rl in enumerate(relays)]
                + [bass.RemoteDMATransfer(dst_ids=[to(hp)], dma_engine_mask=3 << 8 + 2 * q, remote_sem=got[h], src=T.b[4 * h + q], dst=T.b[4 * h + q]) for q, hp in enumerate(helpers)],
                local_sem=S.sent)
        g.wait_ge(S.ld_a, 16)
        rid, pid = topo.addr(r1, core)
        g.remote_dma(T.a[:], T.a[:], S.got0, S.sent, pid, rid, ALL8)
        g.scalar.wait_ge(S.sent, 40)
        g.scalar.dma_start(T.y[:], T.x[:, 0:512]).then_inc(S.st, 16)
        g.wait_ge(S.sent, 40)
        g.wait_ge(S.st, 16)
    elif core in relays or core in helpers:
        if core in relays:
            buf, q, d = (T.c, relays.index(core), r2)
        else:
            buf, q, d = (T.b, helpers.index(core), r3)
        rid, pid = topo.addr(d, core)
        for h in (0, 1):
            g.wait_ge(got[h], 2)
            g.remote_dma(buf[4 * h + q], buf[4 * h + q], got[h], S.sent, pid, rid, ALL8)
        g.wait_ge(S.sent, 16)
    elif core == r1:
        g.sync.wait_ge(S.got0, 8)
        g.sync.dma_start(T.y[:], T.a[:]).then_inc(S.st, 16)
        g.wait_ge(S.st, 16)
    elif core in (r2, r3):
        buf = T.c if core == r2 else T.b
        g.sync.wait_ge(S.got0, 32)
        g.sync.dma_start(T.y[0:64, :], buf[0:4]).then_inc(S.st, 16)
        g.scalar.wait_ge(S.got1, 32)
        g.scalar.dma_start(T.y[64:128, :], buf[4:8]).then_inc(S.st, 16)
        g.wait_ge(S.st, 32)
